import numpy as np
import ml_dtypes


def mxq(x, axis, fmt="e4m3"):
    dtype, down = {"e4m3": (ml_dtypes.float8_e4m3fn, 7), "e5m2": (ml_dtypes.float8_e5m2, 14)}[fmt]
    v = np.moveaxis(np.asarray(x, np.float32).astype(ml_dtypes.bfloat16).astype(np.float64), axis, -1)
    blocks = v.reshape(v.shape[:-1] + (-1, 32))
    amax = np.abs(blocks).max(-1, keepdims=True)
    byte = np.maximum(np.where(amax > 0, np.frexp(amax)[1] - 1 + 127, 0) - down, 1)
    scale = np.exp2(byte - 127.0)
    codes = (blocks / scale).astype(np.float32).astype(dtype).astype(np.float64)
    return np.moveaxis((codes * scale).reshape(v.shape), -1, axis)


WIDE = False


def mx_kscale(k):
    if not WIDE:
        return np.ones(k)
    levels = np.array([10, -10, 5, -5, 0])
    if k % 512:
        return np.exp2(np.random.permutation(np.resize(levels, k // 32))).repeat(32)
    a = np.empty((k // 512, 16))
    for p in range(k // 512):
        a[p, :8] = np.random.permutation(np.resize(levels, 8))
        for g in range(8):
            far = levels[np.abs(levels - a[p, g]) >= 10]
            a[p, g + 8] = far[np.random.randint(len(far))]
    return np.exp2(a.ravel()).repeat(32)


BF16 = ml_dtypes.bfloat16


def bf(x):
    return np.asarray(x, np.float32).astype(BF16)


def f64(x):
    return np.asarray(x).astype(np.float64)


N, X, P, M, E, C, H = 1024, 3, 3, 512, 2, 512, 512
WIDTH2 = 0.0018


def plane_coords(pts):
    u = np.stack([pts[:, 0], pts[:, 0], pts[:, 1]], axis=0)
    v = np.stack([pts[:, 1], pts[:, 2], pts[:, 2]], axis=0)
    return u, v


def softmax_last(s):
    e = np.exp(s - np.max(s, axis=-1, keepdims=True))
    return e / np.sum(e, axis=-1, keepdims=True)


def softplus(t):
    return np.maximum(t, 0.0) + np.log(1.0 + np.exp(-np.abs(t)))


def draw0():
    sm, sc = mx_kscale(M), mx_kscale(C)
    return {
        "pts": bf(np.random.uniform(0.0, 1.0, (N, X))),
        "cen": bf(np.random.uniform(0.0, 1.0, (P, M, E))),
        "ga": bf(np.random.standard_normal((P, M)) * sm),
        "feat": bf(np.random.standard_normal((P, M, C)) * 0.106 * np.sqrt(M) / sm[None, :, None]),
        "gc": bf((1.0 + 0.1 * np.random.standard_normal(C)) * sc),
        "w1": bf(np.random.standard_normal((C, H)) * 2.0 / np.sqrt(C) / sc[:, None]),
        "b1": bf(np.random.standard_normal(H) * 0.4),
    }


def core(pts, cen, ga, feat, gc, w1, b1):
    pts, cen, ga, feat, gc, w1, b1 = f64(pts), f64(cen), f64(ga), f64(feat), f64(gc), f64(w1), f64(b1)
    u, v = plane_coords(pts)
    du = u[:, :, None] - cen[:, None, :, 0]
    dv = v[:, :, None] - cen[:, None, :, 1]
    d2 = du * du + dv * dv
    k = softmax_last(-d2 / WIDTH2)
    a = k * ga[:, None, :]
    f = mxq(a, 2, "e4m3") @ mxq(feat, 1, "e4m3")
    z = f[0] * f[1] * f[2] * gc[None, :]
    t = (mxq(z, 1, "e4m3") @ mxq(w1, 0, "e4m3")) + b1[None, :]
    return softplus(t)


def e4m3fn_bytes(y):
    return np.clip(np.asarray(y, np.float64), -448.0, 448.0).astype(np.float32).astype(ml_dtypes.float8_e4m3fn).view(np.uint8)


def e4m3fn_values(b):
    return np.asarray(b, np.uint8).view(ml_dtypes.float8_e4m3fn).astype(np.float64)


def setup_inputs():
    d = draw0()
    x0 = np.asarray(d['feat']).astype(np.float64)
    s = (np.max(np.abs(x0), axis=(0, 2), keepdims=True) / 448.0).astype(np.float32)
    out = {}
    for k, v in d.items():
        if k == 'feat':
            out['feat_bytes'] = e4m3fn_bytes(x0 / s.astype(np.float64))
            out['feat_scale'] = s
        else:
            out[k] = v
    return out


def reference(pts, cen, ga, feat_bytes, feat_scale, gc, w1, b1):
    return core(pts, cen, ga, e4m3fn_values(feat_bytes) * feat_scale.astype(np.float64), gc, w1, b1)

@@ -1,0 +1,341 @@
+from contextlib import ExitStack
+
+import concourse.mybir as mybir
+from concourse.masks import make_identity
+
+F32 = mybir.dt.float32
+BF16 = mybir.dt.bfloat16
+U32 = mybir.dt.uint32
+U8 = mybir.dt.uint8
+FP8 = mybir.dt.float8_e4m3fn
+FP8X4 = mybir.dt.float8_e4m3fn_x4
+ACT = mybir.ActivationFunctionType
+ALU = mybir.AluOpType
+
+P = 128
+N, X, PLANES, M, C, H = 1024, 3, 3, 512, 512, 512
+T = 4
+WIDTH2 = 0.0018
+BLOCK = 512
+TILES = BLOCK // P
+GROUPS = (N // BLOCK) * PLANES
+UNITS = GROUPS * TILES
+COORDS = ((0, 1), (0, 2), (1, 2))
+CLAMP = 30.0
+
+FLOPS = 2 * N * M * C * PLANES + 2 * N * C * H
+
+
+def tile_kplanesgaussiananchordecoder_kernel(tc, pts, cen, ga, feat_bytes, feat_scale, gc, w1, b1, out):
+    nc = tc.nc
+    with ExitStack() as ctx:
+        keep = ctx.enter_context(tc.tile_pool(name="keep", bufs=1))
+        prep = ctx.enter_context(tc.tile_pool(name="prep", bufs=2))
+        sqp = ctx.enter_context(tc.tile_pool(name="sqp", bufs=2))
+        work = ctx.enter_context(tc.tile_pool(name="work", bufs=3))
+        hold = ctx.enter_context(tc.tile_pool(name="hold", bufs=TILES + 2))
+        late = ctx.enter_context(tc.tile_pool(name="late", bufs=N // P))
+        ps_d = ctx.enter_context(tc.psum_pool(name="ps_d", bufs=2))
+        ps_e = ctx.enter_context(tc.psum_pool(name="ps_e", bufs=2))
+        ps_f = ctx.enter_context(tc.psum_pool(name="ps_f", bufs=2))
+        ps_o = ctx.enter_context(tc.psum_pool(name="ps_o", bufs=2))
+        ctx.enter_context(tc.manual_schedule())
+
+        cen_sb = keep.tile([P, PLANES, T, 2], BF16)
+        nc.sync.dma_start(out=cen_sb[:], in_=cen.rearrange("q (p t) e -> p q t e", t=T))
+        pts_sb = []
+        flat = pts.rearrange("n x -> (n x)")
+        for b in range(N // BLOCK):
+            pb = keep.tile([P, BLOCK, X], BF16, name="pts_%d" % b)
+            pts_sb.append(pb)
+        fb_sb = [keep.tile([P, T, C], U8, name="fbytes_%d" % q) for q in range(PLANES)]
+
+        def load_pts(b):
+            nc.sync.dma_start(
+                out=pts_sb[b][:].rearrange("p n x -> p (n x)"),
+                in_=flat[b * BLOCK * X : (b + 1) * BLOCK * X].partition_broadcast(P),
+            )
+
+        def load_feat(q):
+            nc.sync.dma_start(out=fb_sb[q][:], in_=feat_bytes[q].rearrange("(p t) c -> p t c", t=T))
+
+        load_pts(0)
+        load_feat(0)
+        fs_sb = keep.tile([P, T], F32)
+        nc.sync.dma_start(out=fs_sb[:], in_=feat_scale.rearrange("o (p t) c -> p (o t c)", t=T))
+        ga_sb = keep.tile([P, PLANES, T], BF16)
+        nc.sync.dma_start(out=ga_sb[:], in_=ga.rearrange("q (p t) -> p q t", t=T))
+        load_feat(1)
+        load_pts(1)
+        load_feat(2)
+        w1_raw = keep.tile([P, T, H], BF16)
+        nc.sync.dma_start(out=w1_raw[:], in_=w1.rearrange("(p t) h -> p t h", t=T))
+        gc_sb = keep.tile([P, T], BF16)
+        nc.sync.dma_start(out=gc_sb[:], in_=gc.rearrange("(p t) -> p t", t=T))
+        b1_sb = keep.tile([P, H], BF16)
+        nc.sync.dma_start(out=b1_sb[:], in_=b1.partition_broadcast(P))
+
+        ident = keep.tile([P, P], F32)
+        make_identity(nc, ident[:])
+
+        f_codes = keep.tile([P, PLANES, C], U32, align_bytes=64)
+        f_scales = keep.tile([P, PLANES, C], U8, align_bytes=64)
+        w1_codes = keep.tile([P, H], U32, align_bytes=64)
+        w1_scales = keep.tile([P, H], U8, align_bytes=64)
+        gc_f = keep.tile([P, T], F32)
+
+        wide_t = {}
+        fi_t = {}
+
+        def widen(q):
+            wide = prep.tile([P, T, C], BF16, name="wide")
+            wide_t[q] = wide
+            for t in range(T):
+                nc.vector.tensor_scalar(
+                    out=wide[:, t, :], in0=fb_sb[q][:, t, :].bitcast(FP8),
+                    scalar1=fs_sb[:, t : t + 1], scalar2=None, op0=ALU.mult,
+                )
+
+        def interleave(q, on_vector, parts):
+            if q not in fi_t:
+                fi = prep.tile([P, C, T], BF16, align_bytes=64, name="fi")
+                fi_t[q] = fi
+            dst = fi_t[q][:].rearrange("p (u m) j -> p u m j", u=T)
+            src = wide_t[q][:].rearrange("p j (m u) -> p u m j", u=T)
+            if on_vector:
+                nc.vector.tensor_copy(out=dst, in_=src)
+            else:
+                for u in parts:
+                    nc.gpsimd.tensor_scalar(out=dst[:, u], in0=src[:, u], scalar1=1.0, scalar2=1.0, op0=ALU.mult, op1=ALU.mult)
+
+        def quant_feat(q):
+            nc.vector.quantize_mx(
+                out=f_codes[:, q, :].bitcast(FP8X4), scales=f_scales[:, q, :],
+                in_=fi_t[q][:].rearrange("p c j -> p (c j)"),
+            )
+
+        w1_i = keep.tile([P, H, T], BF16, align_bytes=64)
+
+        def inter_w1(half):
+            cols = slice(half * (H // 2), (half + 1) * (H // 2))
+            nc.gpsimd.tensor_scalar(
+                out=w1_i[:, cols, :], in0=w1_raw[:, :, cols].rearrange("p j h -> p h j"),
+                scalar1=1.0, scalar2=1.0, op0=ALU.mult, op1=ALU.mult,
+            )
+
+        def quant_w1():
+            nc.vector.quantize_mx(
+                out=w1_codes[:].bitcast(FP8X4), scales=w1_scales[:], in_=w1_i[:].rearrange("p h j -> p (h j)"),
+            )
+
+        sq_t = {}
+        d2_t, dn_t, m_t, e_t, s_t, r_t, er_t, et_t, a_t, ac_t, as_t, f_t = ({} for n in range(12))
+        f0_t, g_t, z_t, zc_t, zs_t, o_t, t_t, tcl_t = ({} for n in range(8))
+
+        def where(k):
+            g, i = divmod(k, TILES)
+            b, q = divmod(g, PLANES)
+            return b, q, i
+
+        def squares(g, which, lo, hi):
+            b, q = divmod(g, PLANES)
+            if g not in sq_t:
+                sq = sqp.tile([P, 2, T, BLOCK], F32, name="sq")
+                sq_t[g] = sq
+            for w in which:
+                t, c = divmod(w, 2)
+                nc.scalar.activation(
+                    out=sq_t[g][:, c, t, lo:hi], in_=pts_sb[b][:, lo:hi, COORDS[q][c]],
+                    func=ACT.Square, scale=-1.0, bias=cen_sb[:, q, t, c : c + 1],
+                )
+
+        def dist(k):
+            g, i = divmod(k, TILES)
+            d2 = ps_d.tile([P, T, P], F32, name="d2")
+            d2_t[k] = d2
+            for t in range(T):
+                for c in range(2):
+                    nc.tensor.matmul(
+                        d2[:, t, :], lhsT=sq_t[g][:, c, t, i * P : (i + 1) * P], rhs=ident[:],
+                        start=(c == 0), stop=(c == 1), is_transpose=True,
+                    )
+
+        def minimum(k):
+            dn = work.tile([P, M], F32, name="dn")
+            m = work.tile([P, 1], F32, name="m")
+            dn_t[k], m_t[k] = dn, m
+            nc.vector.tensor_scalar(
+                out=dn[:], in0=d2_t[k][:].rearrange("p t n -> p (t n)"), scalar1=1.0 / WIDTH2, scalar2=None,
+                op0=ALU.mult, op1=ALU.min, accum_out=m[:],
+            )
+
+        def expo(k):
+            e = work.tile([P, M], F32, name="e")
+            s = work.tile([P, 1], F32, name="s")
+            e_t[k], s_t[k] = e, s
+            nc.scalar.activation(out=e[:], in_=dn_t[k][:], func=ACT.Exp, scale=-1.0, bias=m_t[k][:], accum_out=s[:])
+
+        def recip(k):
+            r = work.tile([P, 1], F32, name="r")
+            r_t[k] = r
+            nc.vector.reciprocal(out=r[:], in_=s_t[k][:])
+
+        def norm(k):
+            er = work.tile([P, M], F32, name="er")
+            er_t[k] = er
+            nc.gpsimd.tensor_scalar(out=er[:], in0=e_t[k][:], scalar1=r_t[k][:], scalar2=1.0, op0=ALU.mult, op1=ALU.mult)
+
+        def turn(k):
+            et = ps_e.tile([P, T, P], F32, name="et")
+            et_t[k] = et
+            for t in range(T):
+                nc.tensor.transpose(et[:, t, :], er_t[k][:, t * P : (t + 1) * P], ident[:])
+
+        def gain(k):
+            q = where(k)[1]
+            a = work.tile([P, P, T], BF16, align_bytes=64, name="a")
+            a_t[k] = a
+            nc.vector.tensor_tensor(
+                out=a[:], in0=et_t[k][:].rearrange("p t n -> p n t"),
+                in1=ga_sb[:, q, :].unsqueeze(1).to_broadcast([P, P, T]), op=ALU.mult,
+            )
+
+        def quant_a(k):
+            ac = work.tile([P, P], U32, align_bytes=64, name="ac")
+            asc = work.tile([P, P], U8, align_bytes=64, name="asc")
+            ac_t[k], as_t[k] = ac, asc
+            nc.vector.quantize_mx(out=ac[:].bitcast(FP8X4), scales=asc[:], in_=a_t[k][:].rearrange("p n t -> p (n t)"))
+
+        def feats(k):
+            q = where(k)[1]
+            f = ps_f.tile([P, T, P], F32, name="f")
+            f_t[k] = f
+            for u in range(T):
+                cols = slice(u * P, (u + 1) * P)
+                nc.tensor.matmul_mx(
+                    out=f[:, u, :], lhsT=f_codes[:, q, cols].bitcast(FP8X4), lhsT_scale=f_scales[:, q, cols],
+                    rhs=ac_t[k][:].bitcast(FP8X4), rhs_scale=as_t[k][:], start=True, stop=True,
+                )
+
+        def product(k):
+            b, q, i = where(k)
+            key = b * TILES + i
+            if q == 0:
+                f0 = hold.tile([P, T, P], F32, name="f0")
+                f0_t[key] = f0
+                for u in range(T):
+                    nc.scalar.activation(out=f0[:, u, :], in_=f_t[k][:, u, :], func=ACT.Copy, scale=gc_f[:, u : u + 1])
+            elif q == 1:
+                g = hold.tile([P, T, P], F32, name="g")
+                g_t[key] = g
+                nc.vector.tensor_tensor(out=g[:], in0=f_t[k][:], in1=f0_t[key][:], op=ALU.mult)
+            else:
+                z = work.tile([P, P, T], BF16, align_bytes=64, name="z")
+                z_t[key] = z
+                nc.vector.tensor_tensor(
+                    out=z[:], in0=f_t[k][:].rearrange("p t n -> p n t"), in1=g_t[key][:].rearrange("p t n -> p n t"), op=ALU.mult,
+                )
+
+        def quant_z(key):
+            zc = work.tile([P, P], U32, align_bytes=64, name="zc")
+            zs = work.tile([P, P], U8, align_bytes=64, name="zs")
+            zc_t[key], zs_t[key] = zc, zs
+            nc.vector.quantize_mx(out=zc[:].bitcast(FP8X4), scales=zs[:], in_=z_t[key][:].rearrange("p n t -> p (n t)"))
+
+        def linear(key):
+            o = ps_o.tile([P, H], F32, name="o")
+            o_t[key] = o
+            nc.tensor.matmul_mx(
+                out=o[:], lhsT=zc_t[key][:].bitcast(FP8X4), lhsT_scale=zs_t[key][:],
+                rhs=w1_codes[:].bitcast(FP8X4), rhs_scale=w1_scales[:], start=True, stop=True,
+            )
+
+        def bias(key):
+            tt = late.tile([P, H], F32, name="tt")
+            t_t[key] = tt
+            nc.vector.tensor_tensor(out=tt[:], in0=o_t[key][:], in1=b1_sb[:], op=ALU.add)
+
+        def clamp(key):
+            tl = late.tile([P, H], F32, name="tl")
+            tcl_t[key] = tl
+            nc.gpsimd.tensor_scalar(out=tl[:], in0=t_t[key][:], scalar1=CLAMP, scalar2=-1.0e30, op0=ALU.min, op1=ALU.max)
+
+        def exp_out(key):
+            nc.scalar.activation(out=tcl_t[key][:], in_=tcl_t[key][:], func=ACT.Exp)
+
+        def finish(key):
+            nc.scalar.activation(out=tcl_t[key][:], in_=tcl_t[key][:], func=ACT.Ln, bias=1.0)
+            nc.vector.tensor_max(out=tcl_t[key][:], in0=tcl_t[key][:], in1=t_t[key][:])
+            nc.sync.dma_start(out=out[key * P : (key + 1) * P, :], in_=tcl_t[key][:])
+
+        every = list(range(2 * T))
+        squares(0, every, 0, P)
+        dist(0)
+        widen(0)
+
+        def last(k):
+            return 0 <= k < UNITS and where(k)[1] == PLANES - 1
+
+        def point_tile(k):
+            b, q, i = where(k)
+            return b * TILES + i
+
+        stream = [(g, w) for g in range(1, GROUPS) for w in every]
+        for k in range(UNITS + 6):
+            live = k < UNITS
+            if k < TILES - 1:
+                squares(0, every, (k + 1) * P, (k + 2) * P)
+            if live:
+                minimum(k)
+            ahead = stream[: 3 if k < 2 else 2]
+            stream = stream[len(ahead) :]
+            for g, w in ahead[:1]:
+                squares(g, [w], 0, BLOCK)
+            if live:
+                expo(k)
+            if last(k - 5):
+                exp_out(point_tile(k - 5))
+            if k == 0:
+                nc.vector.tensor_copy(out=gc_f[:], in_=gc_sb[:])
+                interleave(0, True, ())
+            if 0 <= k - 3 < UNITS:
+                product(k - 3)
+            for g, w in ahead[1:]:
+                squares(g, [w], 0, BLOCK)
+            if k + 1 < UNITS:
+                dist(k + 1)
+            if last(k - 4):
+                bias(point_tile(k - 4))
+                clamp(point_tile(k - 4))
+            if 0 <= k - 1 < UNITS:
+                turn(k - 1)
+            if 0 <= k - 2 < UNITS:
+                quant_a(k - 2)
+                feats(k - 2)
+            if last(k - 3):
+                quant_z(point_tile(k - 3))
+                linear(point_tile(k - 3))
+            if 0 <= k - 1 < UNITS:
+                gain(k - 1)
+            if live:
+                recip(k)
+                norm(k)
+            if k == 1:
+                quant_feat(0)
+                widen(1)
+            if k in (2, 3):
+                interleave(1, False, (2 * k - 4, 2 * k - 3))
+            if k == 4:
+                quant_feat(1)
+                widen(2)
+            if k in (5, 6):
+                interleave(2, False, (2 * k - 10, 2 * k - 9))
+            if k in (7, 8):
+                inter_w1(k - 7)
+            if k == 8:
+                quant_feat(2)
+            if k == 9:
+                quant_w1()
+
+        for key in range(N // P):
+            finish(key)

@@ -63,8 +63,9 @@ def tile_kplanesgaussiananchordecoder_kernel(tc, pts, cen, ga, feat_bytes, feat_
         load_feat(0)
         fs_sb = keep.tile([P, T], F32)
         nc.sync.dma_start(out=fs_sb[:], in_=feat_scale.rearrange("o (p t) c -> p (o t c)", t=T))
-        ga_sb = keep.tile([P, PLANES, T], BF16)
-        nc.sync.dma_start(out=ga_sb[:], in_=ga.rearrange("q (p t) -> p q t", t=T))
+        ga_raw = keep.tile([P, PLANES, M], BF16)
+        nc.sync.dma_start(out=ga_raw[:].rearrange("p q m -> p (q m)"), in_=ga.rearrange("q m -> (q m)").partition_broadcast(P))
+        ga_sb = keep.tile([P, PLANES, M], BF16)
         load_feat(1)
         load_pts(1)
         load_feat(2)
@@ -96,17 +97,14 @@ def tile_kplanesgaussiananchordecoder_kernel(tc, pts, cen, ga, feat_bytes, feat_
                     scalar1=fs_sb[:, t : t + 1], scalar2=None, op0=ALU.mult,
                 )
 
-        def interleave(q, on_vector, parts):
+        def interleave(q, parts):
             if q not in fi_t:
                 fi = prep.tile([P, C, T], BF16, align_bytes=64, name="fi")
                 fi_t[q] = fi
             dst = fi_t[q][:].rearrange("p (u m) j -> p u m j", u=T)
             src = wide_t[q][:].rearrange("p j (m u) -> p u m j", u=T)
-            if on_vector:
-                nc.vector.tensor_copy(out=dst, in_=src)
-            else:
-                for u in parts:
-                    nc.gpsimd.tensor_scalar(out=dst[:, u], in0=src[:, u], scalar1=1.0, scalar2=1.0, op0=ALU.mult, op1=ALU.mult)
+            for u in parts:
+                nc.vector.tensor_copy(out=dst[:, u], in_=src[:, u])
 
         def quant_feat(q):
             nc.vector.quantize_mx(
@@ -118,14 +116,17 @@ def tile_kplanesgaussiananchordecoder_kernel(tc, pts, cen, ga, feat_bytes, feat_
 
         def inter_w1(half):
             cols = slice(half * (H // 2), (half + 1) * (H // 2))
-            nc.gpsimd.tensor_scalar(
-                out=w1_i[:, cols, :], in0=w1_raw[:, :, cols].rearrange("p j h -> p h j"),
-                scalar1=1.0, scalar2=1.0, op0=ALU.mult, op1=ALU.mult,
-            )
+            nc.vector.tensor_copy(out=w1_i[:, cols, :], in_=w1_raw[:, :, cols].rearrange("p j h -> p h j"))
 
         def quant_w1():
             nc.vector.quantize_mx(
                 out=w1_codes[:].bitcast(FP8X4), scales=w1_scales[:], in_=w1_i[:].rearrange("p h j -> p (h j)"),
+            )
+
+        def order_gains(q):
+            nc.vector.tensor_copy(
+                out=ga_sb[:, q, :].rearrange("p (u m e) -> p u m e", u=2, e=2),
+                in_=ga_raw[:, q, :].rearrange("p (m u e) -> p u m e", u=2, e=2),
             )
 
         sq_t = {}
@@ -165,7 +166,8 @@ def tile_kplanesgaussiananchordecoder_kernel(tc, pts, cen, ga, feat_bytes, feat_
             m = work.tile([P, 1], F32, name="m")
             dn_t[k], m_t[k] = dn, m
             nc.vector.tensor_scalar(
-                out=dn[:], in0=d2_t[k][:].rearrange("p t n -> p (t n)"), scalar1=1.0 / WIDTH2, scalar2=None,
+                out=dn[:].rearrange("p (u m e) -> p u m e", u=2, e=2),
+                in0=d2_t[k][:].rearrange("p (u e) m -> p u m e", e=2), scalar1=1.0 / WIDTH2, scalar2=None,
                 op0=ALU.mult, op1=ALU.min, accum_out=m[:],
             )
 
@@ -181,23 +183,26 @@ def tile_kplanesgaussiananchordecoder_kernel(tc, pts, cen, ga, feat_bytes, feat_
             nc.vector.reciprocal(out=r[:], in_=s_t[k][:])
 
         def norm(k):
-            er = work.tile([P, M], F32, name="er")
+            q = where(k)[1]
+            er = work.tile([P, M], BF16, align_bytes=64, name="er")
             er_t[k] = er
-            nc.gpsimd.tensor_scalar(out=er[:], in0=e_t[k][:], scalar1=r_t[k][:], scalar2=1.0, op0=ALU.mult, op1=ALU.mult)
+            nc.vector.scalar_tensor_tensor(
+                out=er[:], in0=e_t[k][:], scalar=r_t[k][:], in1=ga_sb[:, q, :], op0=ALU.mult, op1=ALU.mult,
+            )
 
         def turn(k):
-            et = ps_e.tile([P, T, P], F32, name="et")
+            et = ps_e.tile([P, 2, P], F32, name="et")
             et_t[k] = et
-            for t in range(T):
-                nc.tensor.transpose(et[:, t, :], er_t[k][:, t * P : (t + 1) * P], ident[:])
+            words = er_t[k][:].bitcast(F32)
+            for u in range(2):
+                nc.tensor.transpose(et[:, u, :], words[:, u * P : (u + 1) * P], ident[:])
 
-        def gain(k):
-            q = where(k)[1]
+        def gather(k):
             a = work.tile([P, P, T], BF16, align_bytes=64, name="a")
             a_t[k] = a
-            nc.vector.tensor_tensor(
-                out=a[:], in0=et_t[k][:].rearrange("p t n -> p n t"),
-                in1=ga_sb[:, q, :].unsqueeze(1).to_broadcast([P, P, T]), op=ALU.mult,
+            nc.scalar.copy(
+                out=a[:].rearrange("p n t -> p (n t)").bitcast(F32).rearrange("p (n u) -> p n u", u=2),
+                in_=et_t[k][:].rearrange("p u n -> p n u"),
             )
 
         def quant_a(k):
@@ -258,7 +263,7 @@ def tile_kplanesgaussiananchordecoder_kernel(tc, pts, cen, ga, feat_bytes, feat_
         def clamp(key):
             tl = late.tile([P, H], F32, name="tl")
             tcl_t[key] = tl
-            nc.gpsimd.tensor_scalar(out=tl[:], in0=t_t[key][:], scalar1=CLAMP, scalar2=-1.0e30, op0=ALU.min, op1=ALU.max)
+            nc.vector.tensor_scalar(out=tl[:], in0=t_t[key][:], scalar1=CLAMP, scalar2=-1.0e30, op0=ALU.min, op1=ALU.max)
 
         def exp_out(key):
             nc.scalar.activation(out=tcl_t[key][:], in_=tcl_t[key][:], func=ACT.Exp)
@@ -271,65 +276,72 @@ def tile_kplanesgaussiananchordecoder_kernel(tc, pts, cen, ga, feat_bytes, feat_
         every = list(range(2 * T))
         squares(0, every, 0, P)
         dist(0)
+        order_gains(0)
         widen(0)
 
+        def unit(k):
+            return 0 <= k < UNITS
+
         def last(k):
-            return 0 <= k < UNITS and where(k)[1] == PLANES - 1
+            return unit(k) and where(k)[1] == PLANES - 1
 
         def point_tile(k):
             b, q, i = where(k)
             return b * TILES + i
 
         stream = [(g, w) for g in range(1, GROUPS) for w in every]
-        for k in range(UNITS + 6):
-            live = k < UNITS
+        for k in range(UNITS + 7):
+            if unit(k - 2):
+                turn(k - 2)
+                gather(k - 2)
             if k < TILES - 1:
                 squares(0, every, (k + 1) * P, (k + 2) * P)
-            if live:
+            if unit(k):
                 minimum(k)
             ahead = stream[: 3 if k < 2 else 2]
             stream = stream[len(ahead) :]
             for g, w in ahead[:1]:
                 squares(g, [w], 0, BLOCK)
-            if live:
+            if unit(k):
                 expo(k)
-            if last(k - 5):
-                exp_out(point_tile(k - 5))
+            if last(k - 6):
+                exp_out(point_tile(k - 6))
             if k == 0:
                 nc.vector.tensor_copy(out=gc_f[:], in_=gc_sb[:])
-                interleave(0, True, ())
-            if 0 <= k - 3 < UNITS:
-                product(k - 3)
+                interleave(0, range(T))
+            if unit(k - 1):
+                recip(k - 1)
+            if last(k - 5):
+                bias(point_tile(k - 5))
+            if unit(k - 4):
+                product(k - 4)
+            if unit(k + 1):
+                dist(k + 1)
             for g, w in ahead[1:]:
                 squares(g, [w], 0, BLOCK)
-            if k + 1 < UNITS:
-                dist(k + 1)
+            if unit(k - 1):
+                norm(k - 1)
+            if unit(k - 3):
+                quant_a(k - 3)
+                feats(k - 3)
+            if last(k - 5):
+                clamp(point_tile(k - 5))
             if last(k - 4):
-                bias(point_tile(k - 4))
-                clamp(point_tile(k - 4))
-            if 0 <= k - 1 < UNITS:
-                turn(k - 1)
-            if 0 <= k - 2 < UNITS:
-                quant_a(k - 2)
-                feats(k - 2)
-            if last(k - 3):
-                quant_z(point_tile(k - 3))
-                linear(point_tile(k - 3))
-            if 0 <= k - 1 < UNITS:
-                gain(k - 1)
-            if live:
-                recip(k)
-                norm(k)
+                quant_z(point_tile(k - 4))
+                linear(point_tile(k - 4))
             if k == 1:
                 quant_feat(0)
                 widen(1)
+                order_gains(1)
             if k in (2, 3):
-                interleave(1, False, (2 * k - 4, 2 * k - 3))
+                interleave(1, (2 * k - 4, 2 * k - 3))
             if k == 4:
                 quant_feat(1)
                 widen(2)
             if k in (5, 6):
-                interleave(2, False, (2 * k - 10, 2 * k - 9))
+                interleave(2, (2 * k - 10, 2 * k - 9))
+            if k == 6:
+                order_gains(2)
             if k in (7, 8):
                 inter_w1(k - 7)
             if k == 8:

@@ -17,9 +17,11 @@ N, X, PLANES, M, C, H = 1024, 3, 3, 512, 512, 512
 T = 4
 WIDTH2 = 0.0018
 BLOCK = 512
-TILES = BLOCK // P
-GROUPS = (N // BLOCK) * PLANES
-UNITS = GROUPS * TILES
+BLOCKS = ((0, 512), (512, 384), (896, 128))
+GROUPS = [(b, q) for b in range(len(BLOCKS)) for q in range(PLANES)]
+UNIT = [(b, q, i) for b, q in GROUPS for i in range(BLOCKS[b][1] // P)]
+UNITS = len(UNIT)
+FIRST = [UNIT.index((b, q, 0)) for b, q in GROUPS]
 COORDS = ((0, 1), (0, 2), (1, 2))
 CLAMP = 30.0
 
@@ -33,21 +35,20 @@ def tile_kplanesgaussiananchordecoder_kernel(tc, pts, cen, ga, feat_bytes, feat_
         prep = ctx.enter_context(tc.tile_pool(name="prep", bufs=2))
         sqp = ctx.enter_context(tc.tile_pool(name="sqp", bufs=2))
         work = ctx.enter_context(tc.tile_pool(name="work", bufs=3))
-        hold = ctx.enter_context(tc.tile_pool(name="hold", bufs=TILES + 2))
+        hold = ctx.enter_context(tc.tile_pool(name="hold", bufs=6))
         late = ctx.enter_context(tc.tile_pool(name="late", bufs=N // P))
         ps_d = ctx.enter_context(tc.psum_pool(name="ps_d", bufs=2))
         ps_e = ctx.enter_context(tc.psum_pool(name="ps_e", bufs=2))
         ps_f = ctx.enter_context(tc.psum_pool(name="ps_f", bufs=2))
-        ps_o = ctx.enter_context(tc.psum_pool(name="ps_o", bufs=2))
+        ps_o = ctx.enter_context(tc.psum_pool(name="ps_o", bufs=1))
+        ps_w = ctx.enter_context(tc.psum_pool(name="ps_w", bufs=1))
         ctx.enter_context(tc.manual_schedule())
 
         cen_sb = keep.tile([P, PLANES, T, 2], BF16)
         nc.sync.dma_start(out=cen_sb[:], in_=cen.rearrange("q (p t) e -> p q t e", t=T))
-        pts_sb = []
         flat = pts.rearrange("n x -> (n x)")
-        for b in range(N // BLOCK):
-            pb = keep.tile([P, BLOCK, X], BF16, name="pts_%d" % b)
-            pts_sb.append(pb)
+        pts_sb = [keep.tile([P, n, X], BF16, name="pts_%d" % b) for b, (a, n) in enumerate(((0, 512), (512, 512)))]
+        uv_sb = keep.tile([P, X, N], BF16)
         fb_sb = [keep.tile([P, T, C], U8, name="fbytes_%d" % q) for q in range(PLANES)]
 
         def load_pts(b):
@@ -55,6 +56,13 @@ def tile_kplanesgaussiananchordecoder_kernel(tc, pts, cen, ga, feat_bytes, feat_
                 out=pts_sb[b][:].rearrange("p n x -> p (n x)"),
                 in_=flat[b * BLOCK * X : (b + 1) * BLOCK * X].partition_broadcast(P),
             )
+
+        def split_pts(b):
+            for c in range(X):
+                nc.gpsimd.tensor_scalar(
+                    out=uv_sb[:, c, b * BLOCK : (b + 1) * BLOCK], in0=pts_sb[b][:, :, c],
+                    scalar1=1.0, scalar2=1.0, op0=ALU.mult, op1=ALU.mult,
+                )
 
         def load_feat(q):
             nc.sync.dma_start(out=fb_sb[q][:], in_=feat_bytes[q].rearrange("(p t) c -> p t c", t=T))
@@ -134,24 +142,25 @@ def tile_kplanesgaussiananchordecoder_kernel(tc, pts, cen, ga, feat_bytes, feat_
         f0_t, g_t, z_t, zc_t, zs_t, o_t, t_t, tcl_t = ({} for n in range(8))
 
         def where(k):
-            g, i = divmod(k, TILES)
-            b, q = divmod(g, PLANES)
-            return b, q, i
+            return UNIT[k]
 
         def squares(g, which, lo, hi):
-            b, q = divmod(g, PLANES)
+            b, q = GROUPS[g]
+            start = BLOCKS[b][0]
             if g not in sq_t:
                 sq = sqp.tile([P, 2, T, BLOCK], F32, name="sq")
                 sq_t[g] = sq
             for w in which:
                 t, c = divmod(w, 2)
+                x = COORDS[q][c]
                 nc.scalar.activation(
-                    out=sq_t[g][:, c, t, lo:hi], in_=pts_sb[b][:, lo:hi, COORDS[q][c]],
+                    out=sq_t[g][:, c, t, lo:hi], in_=pts_sb[0][:, lo:hi, x] if g == 0 else uv_sb[:, x, start + lo : start + hi],
                     func=ACT.Square, scale=-1.0, bias=cen_sb[:, q, t, c : c + 1],
                 )
 
         def dist(k):
-            g, i = divmod(k, TILES)
+            b, q, i = UNIT[k]
+            g = GROUPS.index((b, q))
             d2 = ps_d.tile([P, T, P], F32, name="d2")
             d2_t[k] = d2
             for t in range(T):
@@ -222,9 +231,16 @@ def tile_kplanesgaussiananchordecoder_kernel(tc, pts, cen, ga, feat_bytes, feat_
                     rhs=ac_t[k][:].bitcast(FP8X4), rhs_scale=as_t[k][:], start=True, stop=True,
                 )
 
+        def warm():
+            w = ps_w.tile([P, C], F32, name="w")
+            nc.tensor.matmul_mx(
+                out=w[:], lhsT=f_codes[:, 0, :P].bitcast(FP8X4), lhsT_scale=f_scales[:, 0, :P],
+                rhs=f_codes[:, 0, :].bitcast(FP8X4), rhs_scale=f_scales[:, 0, :], start=True, stop=True,
+            )
+
         def product(k):
             b, q, i = where(k)
-            key = b * TILES + i
+            key = BLOCKS[b][0] // P + i
             if q == 0:
                 f0 = hold.tile([P, T, P], F32, name="f0")
                 f0_t[key] = f0
@@ -276,8 +292,10 @@ def tile_kplanesgaussiananchordecoder_kernel(tc, pts, cen, ga, feat_bytes, feat_
         every = list(range(2 * T))
         squares(0, every, 0, P)
         dist(0)
-        order_gains(0)
+        split_pts(0)
         widen(0)
+        order_gains(0)
+        split_pts(1)
 
         def unit(k):
             return 0 <= k < UNITS
@@ -287,21 +305,25 @@ def tile_kplanesgaussiananchordecoder_kernel(tc, pts, cen, ga, feat_bytes, feat_
 
         def point_tile(k):
             b, q, i = where(k)
-            return b * TILES + i
+            return BLOCKS[b][0] // P + i
 
-        stream = [(g, w) for g in range(1, GROUPS) for w in every]
+        ahead_of = {}
+        for g in range(1, len(GROUPS)):
+            steps = list(range(max(0, FIRST[g - 1] - 1), FIRST[g] - 1))
+            for w in every:
+                ahead_of.setdefault(steps[w * len(steps) // len(every)], []).append((g, w))
         for k in range(UNITS + 7):
             if unit(k - 2):
                 turn(k - 2)
                 gather(k - 2)
-            if k < TILES - 1:
+            if 0 < k + 1 < FIRST[1]:
                 squares(0, every, (k + 1) * P, (k + 2) * P)
             if unit(k):
                 minimum(k)
-            ahead = stream[: 3 if k < 2 else 2]
-            stream = stream[len(ahead) :]
-            for g, w in ahead[:1]:
-                squares(g, [w], 0, BLOCK)
+            ahead = ahead_of.get(k, [])
+            half = len(ahead) // 2
+            for g, w in ahead[:half]:
+                squares(g, [w], 0, BLOCKS[GROUPS[g][0]][1])
             if unit(k):
                 expo(k)
             if last(k - 6):
@@ -317,13 +339,17 @@ def tile_kplanesgaussiananchordecoder_kernel(tc, pts, cen, ga, feat_bytes, feat_
                 product(k - 4)
             if unit(k + 1):
                 dist(k + 1)
-            for g, w in ahead[1:]:
-                squares(g, [w], 0, BLOCK)
+            if 2 < k < UNITS + 4:
+                warm()
+            for g, w in ahead[half:]:
+                squares(g, [w], 0, BLOCKS[GROUPS[g][0]][1])
             if unit(k - 1):
                 norm(k - 1)
             if unit(k - 3):
                 quant_a(k - 3)
                 feats(k - 3)
+            if 2 < k < UNITS + 4:
+                warm()
             if last(k - 5):
                 clamp(point_tile(k - 5))
             if last(k - 4):

@@ -15,15 +15,48 @@ ALU = mybir.AluOpType
 P = 128
 N, X, PLANES, M, C, H = 1024, 3, 3, 512, 512, 512
 T = 4
+PAIR = 2
+NP = PAIR * P
 WIDTH2 = 0.0018
-BLOCK = 512
-BLOCKS = ((0, 512), (512, 384), (896, 128))
-GROUPS = [(b, q) for b in range(len(BLOCKS)) for q in range(PLANES)]
-UNIT = [(b, q, i) for b, q in GROUPS for i in range(BLOCKS[b][1] // P)]
-UNITS = len(UNIT)
-FIRST = [UNIT.index((b, q, 0)) for b, q in GROUPS]
 COORDS = ((0, 1), (0, 2), (1, 2))
 CLAMP = 30.0
+BLOCKS = ((0, 512), (512, 256), (768, 256))
+GROUPS = [(b, q) for b in range(len(BLOCKS)) for q in range(PLANES)]
+STEPS = [(b, q, j) for b, q in GROUPS for j in range(BLOCKS[b][1] // NP)]
+FIRST = [STEPS.index((b, q, 0)) for b, q in GROUPS]
+NS = len(STEPS)
+
+ORDER = [
+    ("sq0", 0),
+    ("min0", 0),
+    ("exp1", 1),
+    ("gain0", 2),
+    ("recip", 1),
+    ("sq1", 0),
+    ("norm1", 2),
+    ("sq2", 0),
+    ("dist1", 0),
+    ("min1", 0),
+    ("turn1", 2),
+    ("gain1", 2),
+    ("linear", 4),
+    ("feats", 3),
+    ("gz0", 3),
+    ("exp0", 0),
+    ("f0", 3),
+    ("gz1", 3),
+    ("bias", 4),
+    ("prep", 0),
+    ("dist0", -1),
+    ("quanta", 2),
+    ("norm0", 1),
+    ("turn0", 1),
+    ("clamp", 5),
+    ("quantz", 3),
+    ("expout", 6),
+]
+EXTRA = 6
+PREP = {0: "Q0W2W1", 1: "I2Q2", 2: "I1", 3: "Q1I3", 7: "Q3"}
 
 FLOPS = 2 * N * M * C * PLANES + 2 * N * C * H
 
@@ -33,55 +66,46 @@ def tile_kplanesgaussiananchordecoder_kernel(tc, pts, cen, ga, feat_bytes, feat_
     with ExitStack() as ctx:
         keep = ctx.enter_context(tc.tile_pool(name="keep", bufs=1))
         prep = ctx.enter_context(tc.tile_pool(name="prep", bufs=2))
-        sqp = ctx.enter_context(tc.tile_pool(name="sqp", bufs=2))
-        work = ctx.enter_context(tc.tile_pool(name="work", bufs=3))
-        hold = ctx.enter_context(tc.tile_pool(name="hold", bufs=6))
-        late = ctx.enter_context(tc.tile_pool(name="late", bufs=N // P))
+        sqp = ctx.enter_context(tc.tile_pool(name="sqp", bufs=3))
+        work = ctx.enter_context(tc.tile_pool(name="work", bufs=6))
+        mxp = ctx.enter_context(tc.tile_pool(name="mxp", bufs=3))
+        hold = ctx.enter_context(tc.tile_pool(name="hold", bufs=3))
+        late = ctx.enter_context(tc.tile_pool(name="late", bufs=N // NP))
         ps_d = ctx.enter_context(tc.psum_pool(name="ps_d", bufs=2))
         ps_e = ctx.enter_context(tc.psum_pool(name="ps_e", bufs=2))
         ps_f = ctx.enter_context(tc.psum_pool(name="ps_f", bufs=2))
-        ps_o = ctx.enter_context(tc.psum_pool(name="ps_o", bufs=1))
-        ps_w = ctx.enter_context(tc.psum_pool(name="ps_w", bufs=1))
+        ps_o = ctx.enter_context(tc.psum_pool(name="ps_o", bufs=2))
         ctx.enter_context(tc.manual_schedule())
 
         cen_sb = keep.tile([P, PLANES, T, 2], BF16)
-        nc.sync.dma_start(out=cen_sb[:], in_=cen.rearrange("q (p t) e -> p q t e", t=T))
+        pts_sb = keep.tile([P, N, X], BF16)
         flat = pts.rearrange("n x -> (n x)")
-        pts_sb = [keep.tile([P, n, X], BF16, name="pts_%d" % b) for b, (a, n) in enumerate(((0, 512), (512, 512)))]
-        uv_sb = keep.tile([P, X, N], BF16)
         fb_sb = [keep.tile([P, T, C], U8, name="fbytes_%d" % q) for q in range(PLANES)]
+        fs_sb = keep.tile([P, T], F32)
+        ga_sb = keep.tile([P, PLANES, T], BF16)
+        w1_raw = keep.tile([P, T, H], BF16)
+        gc_sb = keep.tile([P, T], BF16)
+        gc_f = keep.tile([P, T], F32)
+        b1_sb = keep.tile([P, H], BF16)
 
-        def load_pts(b):
+        def load_pts(lo, hi):
             nc.sync.dma_start(
-                out=pts_sb[b][:].rearrange("p n x -> p (n x)"),
-                in_=flat[b * BLOCK * X : (b + 1) * BLOCK * X].partition_broadcast(P),
+                out=pts_sb[:, lo:hi, :].rearrange("p n x -> p (n x)"), in_=flat[lo * X : hi * X].partition_broadcast(P),
             )
-
-        def split_pts(b):
-            for c in range(X):
-                nc.gpsimd.tensor_scalar(
-                    out=uv_sb[:, c, b * BLOCK : (b + 1) * BLOCK], in0=pts_sb[b][:, :, c],
-                    scalar1=1.0, scalar2=1.0, op0=ALU.mult, op1=ALU.mult,
-                )
 
         def load_feat(q):
             nc.sync.dma_start(out=fb_sb[q][:], in_=feat_bytes[q].rearrange("(p t) c -> p t c", t=T))
 
-        load_pts(0)
+        nc.sync.dma_start(out=cen_sb[:], in_=cen.rearrange("q (p t) e -> p q t e", t=T))
+        load_pts(0, 256)
         load_feat(0)
-        fs_sb = keep.tile([P, T], F32)
         nc.sync.dma_start(out=fs_sb[:], in_=feat_scale.rearrange("o (p t) c -> p (o t c)", t=T))
-        ga_raw = keep.tile([P, PLANES, M], BF16)
-        nc.sync.dma_start(out=ga_raw[:].rearrange("p q m -> p (q m)"), in_=ga.rearrange("q m -> (q m)").partition_broadcast(P))
-        ga_sb = keep.tile([P, PLANES, M], BF16)
-        load_feat(1)
-        load_pts(1)
-        load_feat(2)
-        w1_raw = keep.tile([P, T, H], BF16)
-        nc.sync.dma_start(out=w1_raw[:], in_=w1.rearrange("(p t) h -> p t h", t=T))
-        gc_sb = keep.tile([P, T], BF16)
+        nc.sync.dma_start(out=ga_sb[:], in_=ga.rearrange("q (p t) -> p q t", t=T))
         nc.sync.dma_start(out=gc_sb[:], in_=gc.rearrange("(p t) -> p t", t=T))
-        b1_sb = keep.tile([P, H], BF16)
+        load_feat(1)
+        load_pts(256, N)
+        load_feat(2)
+        nc.sync.dma_start(out=w1_raw[:], in_=w1.rearrange("(p t) h -> p t h", t=T))
         nc.sync.dma_start(out=b1_sb[:], in_=b1.partition_broadcast(P))
 
         ident = keep.tile([P, P], F32)
@@ -89,12 +113,11 @@ def tile_kplanesgaussiananchordecoder_kernel(tc, pts, cen, ga, feat_bytes, feat_
 
         f_codes = keep.tile([P, PLANES, C], U32, align_bytes=64)
         f_scales = keep.tile([P, PLANES, C], U8, align_bytes=64)
+        w1_i = keep.tile([P, H, T], BF16, align_bytes=64)
         w1_codes = keep.tile([P, H], U32, align_bytes=64)
         w1_scales = keep.tile([P, H], U8, align_bytes=64)
-        gc_f = keep.tile([P, T], F32)
 
-        wide_t = {}
-        fi_t = {}
+        wide_t, fi_t = {}, {}
 
         def widen(q):
             wide = prep.tile([P, T, C], BF16, name="wide")
@@ -105,275 +128,327 @@ def tile_kplanesgaussiananchordecoder_kernel(tc, pts, cen, ga, feat_bytes, feat_
                     scalar1=fs_sb[:, t : t + 1], scalar2=None, op0=ALU.mult,
                 )
 
-        def interleave(q, parts):
-            if q not in fi_t:
-                fi = prep.tile([P, C, T], BF16, align_bytes=64, name="fi")
-                fi_t[q] = fi
-            dst = fi_t[q][:].rearrange("p (u m) j -> p u m j", u=T)
+        def interleave(q, on_vector):
+            fi = prep.tile([P, C, T], BF16, align_bytes=64, name="fi")
+            fi_t[q] = fi
+            dst = fi[:].rearrange("p (u m) j -> p u m j", u=T)
             src = wide_t[q][:].rearrange("p j (m u) -> p u m j", u=T)
-            for u in parts:
-                nc.vector.tensor_copy(out=dst[:, u], in_=src[:, u])
+            if on_vector:
+                nc.vector.tensor_copy(out=dst, in_=src)
+            else:
+                for u in range(T):
+                    nc.gpsimd.tensor_scalar(out=dst[:, u], in0=src[:, u], scalar1=1.0, scalar2=1.0, op0=ALU.mult, op1=ALU.mult)
 
         def quant_feat(q):
             nc.vector.quantize_mx(
-                out=f_codes[:, q, :].bitcast(FP8X4), scales=f_scales[:, q, :],
-                in_=fi_t[q][:].rearrange("p c j -> p (c j)"),
+                out=f_codes[:, q, :].bitcast(FP8X4), scales=f_scales[:, q, :], in_=fi_t[q][:].rearrange("p c j -> p (c j)"),
             )
 
-        w1_i = keep.tile([P, H, T], BF16, align_bytes=64)
-
-        def inter_w1(half):
-            cols = slice(half * (H // 2), (half + 1) * (H // 2))
-            nc.vector.tensor_copy(out=w1_i[:, cols, :], in_=w1_raw[:, :, cols].rearrange("p j h -> p h j"))
+        def inter_w1():
+            for h in range(T):
+                cols = slice(h * P, (h + 1) * P)
+                nc.gpsimd.tensor_scalar(
+                    out=w1_i[:, cols, :], in0=w1_raw[:, :, cols].rearrange("p j h -> p h j"),
+                    scalar1=1.0, scalar2=1.0, op0=ALU.mult, op1=ALU.mult,
+                )
 
         def quant_w1():
             nc.vector.quantize_mx(
                 out=w1_codes[:].bitcast(FP8X4), scales=w1_scales[:], in_=w1_i[:].rearrange("p h j -> p (h j)"),
             )
 
-        def order_gains(q):
-            nc.vector.tensor_copy(
-                out=ga_sb[:, q, :].rearrange("p (u m e) -> p u m e", u=2, e=2),
-                in_=ga_raw[:, q, :].rearrange("p (m u e) -> p u m e", u=2, e=2),
-            )
-
-        sq_t = {}
-        d2_t, dn_t, m_t, e_t, s_t, r_t, er_t, et_t, a_t, ac_t, as_t, f_t = ({} for n in range(12))
-        f0_t, g_t, z_t, zc_t, zs_t, o_t, t_t, tcl_t = ({} for n in range(8))
-
-        def where(k):
-            return UNIT[k]
+        sq_t, d2_t, dn_t, m_t, e_t, s_t, r_t, er_t, et_t, a_t, ac_t, as_t, f_t = ({} for n in range(13))
+        f0_t, g_t, z_t, zc_t, zs_t, o_t, t_t, l_t = ({} for n in range(8))
 
         def squares(g, which, lo, hi):
             b, q = GROUPS[g]
             start = BLOCKS[b][0]
             if g not in sq_t:
-                sq = sqp.tile([P, 2, T, BLOCK], F32, name="sq")
+                sq = sqp.tile([P, 2, T, 512], F32, name="sq")
                 sq_t[g] = sq
             for w in which:
                 t, c = divmod(w, 2)
                 x = COORDS[q][c]
                 nc.scalar.activation(
-                    out=sq_t[g][:, c, t, lo:hi], in_=pts_sb[0][:, lo:hi, x] if g == 0 else uv_sb[:, x, start + lo : start + hi],
+                    out=sq_t[g][:, c, t, lo:hi], in_=pts_sb[:, start + lo : start + hi, x],
                     func=ACT.Square, scale=-1.0, bias=cen_sb[:, q, t, c : c + 1],
                 )
 
-        def dist(k):
-            b, q, i = UNIT[k]
+        def dist(s, i):
+            b, q, j = STEPS[s]
             g = GROUPS.index((b, q))
+            cols = slice(j * NP + i * P, j * NP + (i + 1) * P)
             d2 = ps_d.tile([P, T, P], F32, name="d2")
-            d2_t[k] = d2
+            d2_t[s, i] = d2
             for t in range(T):
                 for c in range(2):
                     nc.tensor.matmul(
-                        d2[:, t, :], lhsT=sq_t[g][:, c, t, i * P : (i + 1) * P], rhs=ident[:],
+                        d2[:, t, :], lhsT=sq_t[g][:, c, t, cols], rhs=ident[:],
                         start=(c == 0), stop=(c == 1), is_transpose=True,
                     )
 
-        def minimum(k):
+        def minimum(s, i):
             dn = work.tile([P, M], F32, name="dn")
             m = work.tile([P, 1], F32, name="m")
-            dn_t[k], m_t[k] = dn, m
+            dn_t[s, i], m_t[s, i] = dn, m
             nc.vector.tensor_scalar(
-                out=dn[:].rearrange("p (u m e) -> p u m e", u=2, e=2),
-                in0=d2_t[k][:].rearrange("p (u e) m -> p u m e", e=2), scalar1=1.0 / WIDTH2, scalar2=None,
+                out=dn[:], in0=d2_t[s, i][:].rearrange("p t n -> p (t n)"), scalar1=1.0 / WIDTH2, scalar2=None,
                 op0=ALU.mult, op1=ALU.min, accum_out=m[:],
             )
 
-        def expo(k):
+        def expo(s, i):
+            if i == 0:
+                total = work.tile([P, PAIR], F32, name="total")
+                s_t[s] = total
             e = work.tile([P, M], F32, name="e")
-            s = work.tile([P, 1], F32, name="s")
-            e_t[k], s_t[k] = e, s
-            nc.scalar.activation(out=e[:], in_=dn_t[k][:], func=ACT.Exp, scale=-1.0, bias=m_t[k][:], accum_out=s[:])
-
-        def recip(k):
-            r = work.tile([P, 1], F32, name="r")
-            r_t[k] = r
-            nc.vector.reciprocal(out=r[:], in_=s_t[k][:])
-
-        def norm(k):
-            q = where(k)[1]
-            er = work.tile([P, M], BF16, align_bytes=64, name="er")
-            er_t[k] = er
-            nc.vector.scalar_tensor_tensor(
-                out=er[:], in0=e_t[k][:], scalar=r_t[k][:], in1=ga_sb[:, q, :], op0=ALU.mult, op1=ALU.mult,
+            e_t[s, i] = e
+            nc.scalar.activation(
+                out=e[:], in_=dn_t[s, i][:], func=ACT.Exp, scale=-1.0, bias=m_t[s, i][:], accum_out=s_t[s][:, i : i + 1],
             )
 
-        def turn(k):
-            et = ps_e.tile([P, 2, P], F32, name="et")
-            et_t[k] = et
-            words = er_t[k][:].bitcast(F32)
-            for u in range(2):
-                nc.tensor.transpose(et[:, u, :], words[:, u * P : (u + 1) * P], ident[:])
+        def recip(s):
+            r = work.tile([P, PAIR], F32, name="r")
+            r_t[s] = r
+            nc.vector.reciprocal(out=r[:], in_=s_t[s][:])
 
-        def gather(k):
-            a = work.tile([P, P, T], BF16, align_bytes=64, name="a")
-            a_t[k] = a
-            nc.scalar.copy(
-                out=a[:].rearrange("p n t -> p (n t)").bitcast(F32).rearrange("p (n u) -> p n u", u=2),
-                in_=et_t[k][:].rearrange("p u n -> p n u"),
+        def norm(s, i):
+            er = work.tile([P, M], F32, name="er")
+            er_t[s, i] = er
+            nc.gpsimd.tensor_scalar(
+                out=er[:], in0=e_t[s, i][:], scalar1=r_t[s][:, i : i + 1], scalar2=1.0, op0=ALU.mult, op1=ALU.mult,
             )
 
-        def quant_a(k):
-            ac = work.tile([P, P], U32, align_bytes=64, name="ac")
-            asc = work.tile([P, P], U8, align_bytes=64, name="asc")
-            ac_t[k], as_t[k] = ac, asc
-            nc.vector.quantize_mx(out=ac[:].bitcast(FP8X4), scales=asc[:], in_=a_t[k][:].rearrange("p n t -> p (n t)"))
+        def turn(s, i):
+            et = ps_e.tile([P, T, P], F32, name="et")
+            et_t[s, i] = et
+            for t in range(T):
+                nc.tensor.transpose(et[:, t, :], er_t[s, i][:, t * P : (t + 1) * P], ident[:])
 
-        def feats(k):
-            q = where(k)[1]
-            f = ps_f.tile([P, T, P], F32, name="f")
-            f_t[k] = f
-            for u in range(T):
-                cols = slice(u * P, (u + 1) * P)
-                nc.tensor.matmul_mx(
-                    out=f[:, u, :], lhsT=f_codes[:, q, cols].bitcast(FP8X4), lhsT_scale=f_scales[:, q, cols],
-                    rhs=ac_t[k][:].bitcast(FP8X4), rhs_scale=as_t[k][:], start=True, stop=True,
-                )
-
-        def warm():
-            w = ps_w.tile([P, C], F32, name="w")
-            nc.tensor.matmul_mx(
-                out=w[:], lhsT=f_codes[:, 0, :P].bitcast(FP8X4), lhsT_scale=f_scales[:, 0, :P],
-                rhs=f_codes[:, 0, :].bitcast(FP8X4), rhs_scale=f_scales[:, 0, :], start=True, stop=True,
+        def gain(s, i):
+            if i == 0:
+                a = mxp.tile([P, NP, T], BF16, align_bytes=64, name="a")
+                a_t[s] = a
+            nc.vector.tensor_tensor(
+                out=a_t[s][:, i * P : (i + 1) * P, :], in0=et_t[s, i][:].rearrange("p t n -> p n t"),
+                in1=ga_sb[:, STEPS[s][1], :].unsqueeze(1).to_broadcast([P, P, T]), op=ALU.mult,
             )
 
-        def product(k):
-            b, q, i = where(k)
-            key = BLOCKS[b][0] // P + i
+        def quant_a(s):
+            ac = mxp.tile([P, NP], U32, align_bytes=64, name="ac")
+            asc = mxp.tile([P, NP], U8, align_bytes=64, name="asc")
+            ac_t[s], as_t[s] = ac, asc
+            nc.vector.quantize_mx(out=ac[:].bitcast(FP8X4), scales=asc[:], in_=a_t[s][:].rearrange("p n t -> p (n t)"))
+
+        def feats(s):
+            q = STEPS[s][1]
+            for h in range(2):
+                if q < 2:
+                    f = ps_f.tile([P, 2, NP], F32, name="f")
+                    todo = [(f[:, u, :], 2 * h + u, slice(0, NP)) for u in range(2)]
+                else:
+                    f = ps_f.tile([P, T, P], F32, name="f")
+                    todo = [(f[:, u, :], u, slice(h * P, (h + 1) * P)) for u in range(T)]
+                f_t[s, h] = f
+                for dst, u, n in todo:
+                    cols = slice(u * P, (u + 1) * P)
+                    nc.tensor.matmul_mx(
+                        out=dst, lhsT=f_codes[:, q, cols].bitcast(FP8X4), lhsT_scale=f_scales[:, q, cols],
+                        rhs=ac_t[s][:, n].bitcast(FP8X4), rhs_scale=as_t[s][:, n], start=True, stop=True,
+                    )
+
+        def pair_of(s):
+            b, q, j = STEPS[s]
+            return BLOCKS[b][0] // NP + j
+
+        def product(s, i):
+            q = STEPS[s][1]
+            key = pair_of(s)
             if q == 0:
-                f0 = hold.tile([P, T, P], F32, name="f0")
+                f0 = hold.tile([P, T, NP], F32, name="f0")
                 f0_t[key] = f0
                 for u in range(T):
-                    nc.scalar.activation(out=f0[:, u, :], in_=f_t[k][:, u, :], func=ACT.Copy, scale=gc_f[:, u : u + 1])
+                    nc.scalar.activation(out=f0[:, u, :], in_=f_t[s, u // 2][:, u % 2, :], func=ACT.Copy, scale=gc_f[:, u : u + 1])
             elif q == 1:
-                g = hold.tile([P, T, P], F32, name="g")
-                g_t[key] = g
-                nc.vector.tensor_tensor(out=g[:], in0=f_t[k][:], in1=f0_t[key][:], op=ALU.mult)
+                if i == 0:
+                    g = hold.tile([P, T, NP], F32, name="g")
+                    g_t[key] = g
+                for h in (i,):
+                    half = slice(2 * h, 2 * h + 2)
+                    nc.vector.tensor_tensor(out=g_t[key][:, half, :], in0=f_t[s, h][:], in1=f0_t[key][:, half, :], op=ALU.mult)
             else:
-                z = work.tile([P, P, T], BF16, align_bytes=64, name="z")
-                z_t[key] = z
-                nc.vector.tensor_tensor(
-                    out=z[:], in0=f_t[k][:].rearrange("p t n -> p n t"), in1=g_t[key][:].rearrange("p t n -> p n t"), op=ALU.mult,
-                )
+                if i == 0:
+                    z = mxp.tile([P, NP, T], BF16, align_bytes=64, name="z")
+                    z_t[key] = z
+                if True:
+                    n = slice(i * P, (i + 1) * P)
+                    nc.vector.tensor_tensor(
+                        out=z_t[key][:, n, :], in0=f_t[s, i][:].rearrange("p t n -> p n t"),
+                        in1=g_t[key][:, :, n].rearrange("p t n -> p n t"), op=ALU.mult,
+                    )
+
+        def pieces(key):
+            return [slice(0, PAIR)] if key < N // NP - 1 else [slice(i, i + 1) for i in range(PAIR)]
 
         def quant_z(key):
-            zc = work.tile([P, P], U32, align_bytes=64, name="zc")
-            zs = work.tile([P, P], U8, align_bytes=64, name="zs")
+            zc = mxp.tile([P, NP], U32, align_bytes=64, name="zc")
+            zs = mxp.tile([P, NP], U8, align_bytes=64, name="zs")
             zc_t[key], zs_t[key] = zc, zs
-            nc.vector.quantize_mx(out=zc[:].bitcast(FP8X4), scales=zs[:], in_=z_t[key][:].rearrange("p n t -> p (n t)"))
+            for i in pieces(key):
+                n = slice(i.start * P, i.stop * P)
+                nc.vector.quantize_mx(out=zc[:, n].bitcast(FP8X4), scales=zs[:, n], in_=z_t[key][:, n, :].rearrange("p n t -> p (n t)"))
 
         def linear(key):
-            o = ps_o.tile([P, H], F32, name="o")
-            o_t[key] = o
-            nc.tensor.matmul_mx(
-                out=o[:], lhsT=zc_t[key][:].bitcast(FP8X4), lhsT_scale=zs_t[key][:],
-                rhs=w1_codes[:].bitcast(FP8X4), rhs_scale=w1_scales[:], start=True, stop=True,
-            )
+            for i in range(PAIR):
+                o = ps_o.tile([P, H], F32, name="o")
+                o_t[key, i] = o
+                n = slice(i * P, (i + 1) * P)
+                nc.tensor.matmul_mx(
+                    out=o[:], lhsT=zc_t[key][:, n].bitcast(FP8X4), lhsT_scale=zs_t[key][:, n],
+                    rhs=w1_codes[:].bitcast(FP8X4), rhs_scale=w1_scales[:], start=True, stop=True,
+                )
 
         def bias(key):
-            tt = late.tile([P, H], F32, name="tt")
+            tt = late.tile([P, PAIR, H], F32, name="tt")
             t_t[key] = tt
-            nc.vector.tensor_tensor(out=tt[:], in0=o_t[key][:], in1=b1_sb[:], op=ALU.add)
+            for i in range(PAIR):
+                nc.vector.tensor_tensor(out=tt[:, i, :], in0=o_t[key, i][:], in1=b1_sb[:], op=ALU.add)
 
         def clamp(key):
-            tl = late.tile([P, H], F32, name="tl")
-            tcl_t[key] = tl
-            nc.vector.tensor_scalar(out=tl[:], in0=t_t[key][:], scalar1=CLAMP, scalar2=-1.0e30, op0=ALU.min, op1=ALU.max)
+            lt = late.tile([P, PAIR, H], F32, name="lt")
+            l_t[key] = lt
+            if key < N // NP - 1:
+                nc.gpsimd.tensor_scalar(out=lt[:], in0=t_t[key][:], scalar1=CLAMP, scalar2=-1.0e30, op0=ALU.min, op1=ALU.max)
+            else:
+                for i in range(PAIR):
+                    nc.vector.tensor_scalar(out=lt[:, i, :], in0=t_t[key][:, i, :], scalar1=CLAMP, scalar2=None, op0=ALU.min)
 
         def exp_out(key):
-            nc.scalar.activation(out=tcl_t[key][:], in_=tcl_t[key][:], func=ACT.Exp)
+            for i in pieces(key):
+                nc.scalar.activation(out=l_t[key][:, i, :], in_=l_t[key][:, i, :], func=ACT.Exp)
 
-        def finish(key):
-            nc.scalar.activation(out=tcl_t[key][:], in_=tcl_t[key][:], func=ACT.Ln, bias=1.0)
-            nc.vector.tensor_max(out=tcl_t[key][:], in0=tcl_t[key][:], in1=t_t[key][:])
-            nc.sync.dma_start(out=out[key * P : (key + 1) * P, :], in_=tcl_t[key][:])
+        def log_out(key, i):
+            nc.scalar.activation(out=l_t[key][:, i, :], in_=l_t[key][:, i, :], func=ACT.Ln, bias=1.0)
+
+        def finish(key, i):
+            nc.vector.tensor_max(out=l_t[key][:, i, :], in0=l_t[key][:, i, :], in1=t_t[key][:, i, :])
+            n0 = (key * PAIR + i.start) * P
+            n1 = (key * PAIR + i.stop) * P
+            nc.sync.dma_start(out=out[n0:n1, :].rearrange("(i p) h -> p i h", p=P), in_=l_t[key][:, i, :])
 
         every = list(range(2 * T))
         squares(0, every, 0, P)
-        dist(0)
-        split_pts(0)
+        dist(0, 0)
+        squares(0, every, P, NP)
+        dist(0, 1)
         widen(0)
-        order_gains(0)
-        split_pts(1)
+        interleave(0, True)
+        nc.gpsimd.tensor_scalar(out=gc_f[:], in0=gc_sb[:], scalar1=1.0, scalar2=1.0, op0=ALU.mult, op1=ALU.mult)
 
-        def unit(k):
-            return 0 <= k < UNITS
+        def live(s):
+            return 0 <= s < NS
 
-        def last(k):
-            return unit(k) and where(k)[1] == PLANES - 1
+        def last(s):
+            return live(s) and STEPS[s][1] == PLANES - 1
 
-        def point_tile(k):
-            b, q, i = where(k)
-            return BLOCKS[b][0] // P + i
+        todo = [(0, w, NP, 2 * NP) for w in every] + [
+            (g, w, 0, BLOCKS[GROUPS[g][0]][1]) for g in range(1, len(GROUPS)) for w in every
+        ]
+        total = sum([hi - lo for g, w, lo, hi in todo])
+        ahead_of, cum = {}, 0
+        for s in range(NS - 1):
+            due = sum([hi - lo for g, w, lo, hi in todo if FIRST[g] <= s + 1])
+            target = max(due, total * (s + 1) / (NS - 1) - cum)
+            ahead_of[s] = []
+            spent = 0
+            while todo and spent < target and (todo[0][0] < 3 or FIRST[todo[0][0] - 2] <= s):
+                ahead_of[s].append(todo[0])
+                spent = spent + todo[0][3] - todo[0][2]
+                todo = todo[1:]
+            cum = cum + spent
 
-        ahead_of = {}
-        for g in range(1, len(GROUPS)):
-            steps = list(range(max(0, FIRST[g - 1] - 1), FIRST[g] - 1))
-            for w in every:
-                ahead_of.setdefault(steps[w * len(steps) // len(every)], []).append((g, w))
-        for k in range(UNITS + 7):
-            if unit(k - 2):
-                turn(k - 2)
-                gather(k - 2)
-            if 0 < k + 1 < FIRST[1]:
-                squares(0, every, (k + 1) * P, (k + 2) * P)
-            if unit(k):
-                minimum(k)
-            ahead = ahead_of.get(k, [])
-            half = len(ahead) // 2
-            for g, w in ahead[:half]:
-                squares(g, [w], 0, BLOCKS[GROUPS[g][0]][1])
-            if unit(k):
-                expo(k)
-            if last(k - 6):
-                exp_out(point_tile(k - 6))
-            if k == 0:
-                nc.vector.tensor_copy(out=gc_f[:], in_=gc_sb[:])
-                interleave(0, range(T))
-            if unit(k - 1):
-                recip(k - 1)
-            if last(k - 5):
-                bias(point_tile(k - 5))
-            if unit(k - 4):
-                product(k - 4)
-            if unit(k + 1):
-                dist(k + 1)
-            if 2 < k < UNITS + 4:
-                warm()
-            for g, w in ahead[half:]:
-                squares(g, [w], 0, BLOCKS[GROUPS[g][0]][1])
-            if unit(k - 1):
-                norm(k - 1)
-            if unit(k - 3):
-                quant_a(k - 3)
-                feats(k - 3)
-            if 2 < k < UNITS + 4:
-                warm()
-            if last(k - 5):
-                clamp(point_tile(k - 5))
-            if last(k - 4):
-                quant_z(point_tile(k - 4))
-                linear(point_tile(k - 4))
-            if k == 1:
-                quant_feat(0)
-                widen(1)
-                order_gains(1)
-            if k in (2, 3):
-                interleave(1, (2 * k - 4, 2 * k - 3))
-            if k == 4:
-                quant_feat(1)
-                widen(2)
-            if k in (5, 6):
-                interleave(2, (2 * k - 10, 2 * k - 9))
-            if k == 6:
-                order_gains(2)
-            if k in (7, 8):
-                inter_w1(k - 7)
-            if k == 8:
-                quant_feat(2)
-            if k == 9:
-                quant_w1()
+        both = slice(0, PAIR)
+        def prep_step(s):
+            todo = PREP.get(s, "")
+            for j in range(0, len(todo), 2):
+                what, q = todo[j], int(todo[j + 1])
+                if what == "W":
+                    widen(q)
+                elif what == "I":
+                    if q == 3:
+                        inter_w1()
+                    else:
+                        interleave(q, False)
+                elif what == "J":
+                    interleave(q, True)
+                elif what == "Q":
+                    if q == 3:
+                        quant_w1()
+                    else:
+                        quant_feat(q)
 
-        for key in range(N // P):
-            finish(key)
+        done_sq = [0]
+        for s in range(NS + EXTRA):
+            ahead = ahead_of.get(s, [])
+            for token, lag in ORDER:
+                k = s - lag
+                name, i = (token[:-1], int(token[-1])) if token[-1] in "012" else (token, 0)
+                if token == "f0":
+                    name, i = token, 0
+                if name == "sq":
+                    n = len(ahead)
+                    for g, w, lo, hi in ahead[i * n // 3 : (i + 1) * n // 3]:
+                        squares(g, [w], lo, hi)
+                    continue
+                if name == "prep":
+                    prep_step(s)
+                    continue
+                if not live(k):
+                    continue
+                q = STEPS[k][1]
+                if name == "turn":
+                    turn(k, i)
+                elif name == "min":
+                    minimum(k, i)
+                elif name == "exp":
+                    expo(k, i)
+                elif name == "dist":
+                    if k > 0:
+                        dist(k, i)
+                elif name == "norm":
+                    norm(k, i)
+                elif name == "recip":
+                    recip(k)
+                elif name == "gain":
+                    gain(k, i)
+                elif name == "quanta":
+                    quant_a(k)
+                elif name == "feats":
+                    feats(k)
+                elif name == "f0":
+                    if q == 0:
+                        product(k, 0)
+                elif name == "gz":
+                    if q > 0:
+                        product(k, i)
+                elif q == 2:
+                    key = pair_of(k)
+                    if name == "quantz":
+                        quant_z(key)
+                    elif name == "linear":
+                        linear(key)
+                    elif name == "bias":
+                        bias(key)
+                    elif name == "clamp":
+                        clamp(key)
+                    elif name == "expout":
+                        if key < N // NP - 1:
+                            exp_out(key)
+
+        pairs = N // NP
+        for key in range(pairs - 1):
+            log_out(key, both)
+            finish(key, both)
+        exp_out(pairs - 1)
+        for i in range(PAIR):
+            log_out(pairs - 1, slice(i, i + 1))
+            finish(pairs - 1, slice(i, i + 1))

from contextlib import ExitStack

import concourse.mybir as mybir
from concourse.masks import make_identity

F32 = mybir.dt.float32
BF16 = mybir.dt.bfloat16
U32 = mybir.dt.uint32
U8 = mybir.dt.uint8
FP8 = mybir.dt.float8_e4m3fn
FP8X4 = mybir.dt.float8_e4m3fn_x4
ACT = mybir.ActivationFunctionType
ALU = mybir.AluOpType

P = 128
N, X, PLANES, M, C, H = 1024, 3, 3, 512, 512, 512
T = 4
PAIR = 2
NP = PAIR * P
WIDTH2 = 0.0018
COORDS = ((0, 1), (0, 2), (1, 2))
CLAMP = 30.0
BLOCKS = ((0, 512), (512, 256), (768, 256))
GROUPS = [(b, q) for b in range(len(BLOCKS)) for q in range(PLANES)]
STEPS = [(b, q, j) for b, q in GROUPS for j in range(BLOCKS[b][1] // NP)]
FIRST = [STEPS.index((b, q, 0)) for b, q in GROUPS]
NS = len(STEPS)

ORDER = [
    ("sq0", 0),
    ("min0", 0),
    ("exp1", 1),
    ("gain0", 2),
    ("recip", 1),
    ("sq1", 0),
    ("norm1", 2),
    ("sq2", 0),
    ("dist1", 0),
    ("min1", 0),
    ("turn1", 2),
    ("gain1", 2),
    ("linear", 4),
    ("feats", 3),
    ("gz0", 3),
    ("exp0", 0),
    ("f0", 3),
    ("gz1", 3),
    ("bias", 4),
    ("prep", 0),
    ("dist0", -1),
    ("quanta", 2),
    ("norm0", 1),
    ("turn0", 1),
    ("clamp", 5),
    ("quantz", 3),
    ("expout", 6),
]
EXTRA = 6
PREP = {0: "Q0W2W1", 1: "I2Q2", 2: "I1", 3: "Q1I3", 7: "Q3"}

FLOPS = 2 * N * M * C * PLANES + 2 * N * C * H


def tile_kplanesgaussiananchordecoder_kernel(tc, pts, cen, ga, feat_bytes, feat_scale, gc, w1, b1, out):
    nc = tc.nc
    with ExitStack() as ctx:
        keep = ctx.enter_context(tc.tile_pool(name="keep", bufs=1))
        prep = ctx.enter_context(tc.tile_pool(name="prep", bufs=2))
        sqp = ctx.enter_context(tc.tile_pool(name="sqp", bufs=3))
        work = ctx.enter_context(tc.tile_pool(name="work", bufs=6))
        mxp = ctx.enter_context(tc.tile_pool(name="mxp", bufs=3))
        hold = ctx.enter_context(tc.tile_pool(name="hold", bufs=3))
        late = ctx.enter_context(tc.tile_pool(name="late", bufs=N // NP))
        ps_d = ctx.enter_context(tc.psum_pool(name="ps_d", bufs=2))
        ps_e = ctx.enter_context(tc.psum_pool(name="ps_e", bufs=2))
        ps_f = ctx.enter_context(tc.psum_pool(name="ps_f", bufs=2))
        ps_o = ctx.enter_context(tc.psum_pool(name="ps_o", bufs=2))
        ctx.enter_context(tc.manual_schedule())

        cen_sb = keep.tile([P, PLANES, T, 2], BF16)
        pts_sb = keep.tile([P, N, X], BF16)
        flat = pts.rearrange("n x -> (n x)")
        fb_sb = [keep.tile([P, T, C], U8, name="fbytes_%d" % q) for q in range(PLANES)]
        fs_sb = keep.tile([P, T], F32)
        ga_sb = keep.tile([P, PLANES, T], BF16)
        w1_raw = keep.tile([P, T, H], BF16)
        gc_sb = keep.tile([P, T], BF16)
        gc_f = keep.tile([P, T], F32)
        b1_sb = keep.tile([P, H], BF16)

        def load_pts(lo, hi):
            nc.sync.dma_start(
                out=pts_sb[:, lo:hi, :].rearrange("p n x -> p (n x)"), in_=flat[lo * X : hi * X].partition_broadcast(P),
            )

        def load_feat(q):
            nc.sync.dma_start(out=fb_sb[q][:], in_=feat_bytes[q].rearrange("(p t) c -> p t c", t=T))

        nc.sync.dma_start(out=cen_sb[:], in_=cen.rearrange("q (p t) e -> p q t e", t=T))
        load_pts(0, 256)
        load_feat(0)
        nc.sync.dma_start(out=fs_sb[:], in_=feat_scale.rearrange("o (p t) c -> p (o t c)", t=T))
        nc.sync.dma_start(out=ga_sb[:], in_=ga.rearrange("q (p t) -> p q t", t=T))
        nc.sync.dma_start(out=gc_sb[:], in_=gc.rearrange("(p t) -> p t", t=T))
        load_feat(1)
        load_pts(256, N)
        load_feat(2)
        nc.sync.dma_start(out=w1_raw[:], in_=w1.rearrange("(p t) h -> p t h", t=T))
        nc.sync.dma_start(out=b1_sb[:], in_=b1.partition_broadcast(P))

        ident = keep.tile([P, P], F32)
        make_identity(nc, ident[:])

        f_codes = keep.tile([P, PLANES, C], U32, align_bytes=64)
        f_scales = keep.tile([P, PLANES, C], U8, align_bytes=64)
        w1_i = keep.tile([P, H, T], BF16, align_bytes=64)
        w1_codes = keep.tile([P, H], U32, align_bytes=64)
        w1_scales = keep.tile([P, H], U8, align_bytes=64)

        wide_t, fi_t = {}, {}

        def widen(q):
            wide = prep.tile([P, T, C], BF16, name="wide")
            wide_t[q] = wide
            for t in range(T):
                nc.vector.tensor_scalar(
                    out=wide[:, t, :], in0=fb_sb[q][:, t, :].bitcast(FP8),
                    scalar1=fs_sb[:, t : t + 1], scalar2=None, op0=ALU.mult,
                )

        def interleave(q, on_vector):
            fi = prep.tile([P, C, T], BF16, align_bytes=64, name="fi")
            fi_t[q] = fi
            dst = fi[:].rearrange("p (u m) j -> p u m j", u=T)
            src = wide_t[q][:].rearrange("p j (m u) -> p u m j", u=T)
            if on_vector:
                nc.vector.tensor_copy(out=dst, in_=src)
            else:
                for u in range(T):
                    nc.gpsimd.tensor_scalar(out=dst[:, u], in0=src[:, u], scalar1=1.0, scalar2=1.0, op0=ALU.mult, op1=ALU.mult)

        def quant_feat(q):
            nc.vector.quantize_mx(
                out=f_codes[:, q, :].bitcast(FP8X4), scales=f_scales[:, q, :], in_=fi_t[q][:].rearrange("p c j -> p (c j)"),
            )

        def inter_w1():
            for h in range(T):
                cols = slice(h * P, (h + 1) * P)
                nc.gpsimd.tensor_scalar(
                    out=w1_i[:, cols, :], in0=w1_raw[:, :, cols].rearrange("p j h -> p h j"),
                    scalar1=1.0, scalar2=1.0, op0=ALU.mult, op1=ALU.mult,
                )

        def quant_w1():
            nc.vector.quantize_mx(
                out=w1_codes[:].bitcast(FP8X4), scales=w1_scales[:], in_=w1_i[:].rearrange("p h j -> p (h j)"),
            )

        sq_t, d2_t, dn_t, m_t, e_t, s_t, r_t, er_t, et_t, a_t, ac_t, as_t, f_t = ({} for n in range(13))
        f0_t, g_t, z_t, zc_t, zs_t, o_t, t_t, l_t = ({} for n in range(8))

        def squares(g, which, lo, hi):
            b, q = GROUPS[g]
            start = BLOCKS[b][0]
            if g not in sq_t:
                sq = sqp.tile([P, 2, T, 512], F32, name="sq")
                sq_t[g] = sq
            for w in which:
                t, c = divmod(w, 2)
                x = COORDS[q][c]
                nc.scalar.activation(
                    out=sq_t[g][:, c, t, lo:hi], in_=pts_sb[:, start + lo : start + hi, x],
                    func=ACT.Square, scale=-1.0, bias=cen_sb[:, q, t, c : c + 1],
                )

        def dist(s, i):
            b, q, j = STEPS[s]
            g = GROUPS.index((b, q))
            cols = slice(j * NP + i * P, j * NP + (i + 1) * P)
            d2 = ps_d.tile([P, T, P], F32, name="d2")
            d2_t[s, i] = d2
            for t in range(T):
                for c in range(2):
                    nc.tensor.matmul(
                        d2[:, t, :], lhsT=sq_t[g][:, c, t, cols], rhs=ident[:],
                        start=(c == 0), stop=(c == 1), is_transpose=True,
                    )

        def minimum(s, i):
            dn = work.tile([P, M], F32, name="dn")
            m = work.tile([P, 1], F32, name="m")
            dn_t[s, i], m_t[s, i] = dn, m
            nc.vector.tensor_scalar(
                out=dn[:], in0=d2_t[s, i][:].rearrange("p t n -> p (t n)"), scalar1=1.0 / WIDTH2, scalar2=None,
                op0=ALU.mult, op1=ALU.min, accum_out=m[:],
            )

        def expo(s, i):
            if i == 0:
                total = work.tile([P, PAIR], F32, name="total")
                s_t[s] = total
            e = work.tile([P, M], F32, name="e")
            e_t[s, i] = e
            nc.scalar.activation(
                out=e[:], in_=dn_t[s, i][:], func=ACT.Exp, scale=-1.0, bias=m_t[s, i][:], accum_out=s_t[s][:, i : i + 1],
            )

        def recip(s):
            r = work.tile([P, PAIR], F32, name="r")
            r_t[s] = r
            nc.vector.reciprocal(out=r[:], in_=s_t[s][:])

        def norm(s, i):
            er = work.tile([P, M], F32, name="er")
            er_t[s, i] = er
            nc.gpsimd.tensor_scalar(
                out=er[:], in0=e_t[s, i][:], scalar1=r_t[s][:, i : i + 1], scalar2=1.0, op0=ALU.mult, op1=ALU.mult,
            )

        def turn(s, i):
            et = ps_e.tile([P, T, P], F32, name="et")
            et_t[s, i] = et
            for t in range(T):
                nc.tensor.transpose(et[:, t, :], er_t[s, i][:, t * P : (t + 1) * P], ident[:])

        def gain(s, i):
            if i == 0:
                a = mxp.tile([P, NP, T], BF16, align_bytes=64, name="a")
                a_t[s] = a
            nc.vector.tensor_tensor(
                out=a_t[s][:, i * P : (i + 1) * P, :], in0=et_t[s, i][:].rearrange("p t n -> p n t"),
                in1=ga_sb[:, STEPS[s][1], :].unsqueeze(1).to_broadcast([P, P, T]), op=ALU.mult,
            )

        def quant_a(s):
            ac = mxp.tile([P, NP], U32, align_bytes=64, name="ac")
            asc = mxp.tile([P, NP], U8, align_bytes=64, name="asc")
            ac_t[s], as_t[s] = ac, asc
            nc.vector.quantize_mx(out=ac[:].bitcast(FP8X4), scales=asc[:], in_=a_t[s][:].rearrange("p n t -> p (n t)"))

        def feats(s):
            q = STEPS[s][1]
            for h in range(2):
                if q < 2:
                    f = ps_f.tile([P, 2, NP], F32, name="f")
                    todo = [(f[:, u, :], 2 * h + u, slice(0, NP)) for u in range(2)]
                else:
                    f = ps_f.tile([P, T, P], F32, name="f")
                    todo = [(f[:, u, :], u, slice(h * P, (h + 1) * P)) for u in range(T)]
                f_t[s, h] = f
                for dst, u, n in todo:
                    cols = slice(u * P, (u + 1) * P)
                    nc.tensor.matmul_mx(
                        out=dst, lhsT=f_codes[:, q, cols].bitcast(FP8X4), lhsT_scale=f_scales[:, q, cols],
                        rhs=ac_t[s][:, n].bitcast(FP8X4), rhs_scale=as_t[s][:, n], start=True, stop=True,
                    )

        def pair_of(s):
            b, q, j = STEPS[s]
            return BLOCKS[b][0] // NP + j

        def product(s, i):
            q = STEPS[s][1]
            key = pair_of(s)
            if q == 0:
                f0 = hold.tile([P, T, NP], F32, name="f0")
                f0_t[key] = f0
                for u in range(T):
                    nc.scalar.activation(out=f0[:, u, :], in_=f_t[s, u // 2][:, u % 2, :], func=ACT.Copy, scale=gc_f[:, u : u + 1])
            elif q == 1:
                if i == 0:
                    g = hold.tile([P, T, NP], F32, name="g")
                    g_t[key] = g
                for h in (i,):
                    half = slice(2 * h, 2 * h + 2)
                    nc.vector.tensor_tensor(out=g_t[key][:, half, :], in0=f_t[s, h][:], in1=f0_t[key][:, half, :], op=ALU.mult)
            else:
                if i == 0:
                    z = mxp.tile([P, NP, T], BF16, align_bytes=64, name="z")
                    z_t[key] = z
                if True:
                    n = slice(i * P, (i + 1) * P)
                    nc.vector.tensor_tensor(
                        out=z_t[key][:, n, :], in0=f_t[s, i][:].rearrange("p t n -> p n t"),
                        in1=g_t[key][:, :, n].rearrange("p t n -> p n t"), op=ALU.mult,
                    )

        def pieces(key):
            return [slice(0, PAIR)] if key < N // NP - 1 else [slice(i, i + 1) for i in range(PAIR)]

        def quant_z(key):
            zc = mxp.tile([P, NP], U32, align_bytes=64, name="zc")
            zs = mxp.tile([P, NP], U8, align_bytes=64, name="zs")
            zc_t[key], zs_t[key] = zc, zs
            for i in pieces(key):
                n = slice(i.start * P, i.stop * P)
                nc.vector.quantize_mx(out=zc[:, n].bitcast(FP8X4), scales=zs[:, n], in_=z_t[key][:, n, :].rearrange("p n t -> p (n t)"))

        def linear(key):
            for i in range(PAIR):
                o = ps_o.tile([P, H], F32, name="o")
                o_t[key, i] = o
                n = slice(i * P, (i + 1) * P)
                nc.tensor.matmul_mx(
                    out=o[:], lhsT=zc_t[key][:, n].bitcast(FP8X4), lhsT_scale=zs_t[key][:, n],
                    rhs=w1_codes[:].bitcast(FP8X4), rhs_scale=w1_scales[:], start=True, stop=True,
                )

        def bias(key):
            tt = late.tile([P, PAIR, H], F32, name="tt")
            t_t[key] = tt
            for i in range(PAIR):
                nc.vector.tensor_tensor(out=tt[:, i, :], in0=o_t[key, i][:], in1=b1_sb[:], op=ALU.add)

        def clamp(key):
            lt = late.tile([P, PAIR, H], F32, name="lt")
            l_t[key] = lt
            if key < N // NP - 1:
                nc.gpsimd.tensor_scalar(out=lt[:], in0=t_t[key][:], scalar1=CLAMP, scalar2=-1.0e30, op0=ALU.min, op1=ALU.max)
            else:
                for i in range(PAIR):
                    nc.vector.tensor_scalar(out=lt[:, i, :], in0=t_t[key][:, i, :], scalar1=CLAMP, scalar2=None, op0=ALU.min)

        def exp_out(key):
            for i in pieces(key):
                nc.scalar.activation(out=l_t[key][:, i, :], in_=l_t[key][:, i, :], func=ACT.Exp)

        def log_out(key, i):
            nc.scalar.activation(out=l_t[key][:, i, :], in_=l_t[key][:, i, :], func=ACT.Ln, bias=1.0)

        def finish(key, i):
            nc.vector.tensor_max(out=l_t[key][:, i, :], in0=l_t[key][:, i, :], in1=t_t[key][:, i, :])
            n0 = (key * PAIR + i.start) * P
            n1 = (key * PAIR + i.stop) * P
            nc.sync.dma_start(out=out[n0:n1, :].rearrange("(i p) h -> p i h", p=P), in_=l_t[key][:, i, :])

        every = list(range(2 * T))
        squares(0, every, 0, P)
        dist(0, 0)
        squares(0, every, P, NP)
        dist(0, 1)
        widen(0)
        interleave(0, True)
        nc.gpsimd.tensor_scalar(out=gc_f[:], in0=gc_sb[:], scalar1=1.0, scalar2=1.0, op0=ALU.mult, op1=ALU.mult)

        def live(s):
            return 0 <= s < NS

        def last(s):
            return live(s) and STEPS[s][1] == PLANES - 1

        todo = [(0, w, NP, 2 * NP) for w in every] + [
            (g, w, 0, BLOCKS[GROUPS[g][0]][1]) for g in range(1, len(GROUPS)) for w in every
        ]
        total = sum([hi - lo for g, w, lo, hi in todo])
        ahead_of, cum = {}, 0
        for s in range(NS - 1):
            due = sum([hi - lo for g, w, lo, hi in todo if FIRST[g] <= s + 1])
            target = max(due, total * (s + 1) / (NS - 1) - cum)
            ahead_of[s] = []
            spent = 0
            while todo and spent < target and (todo[0][0] < 3 or FIRST[todo[0][0] - 2] <= s):
                ahead_of[s].append(todo[0])
                spent = spent + todo[0][3] - todo[0][2]
                todo = todo[1:]
            cum = cum + spent

        both = slice(0, PAIR)
        def prep_step(s):
            todo = PREP.get(s, "")
            for j in range(0, len(todo), 2):
                what, q = todo[j], int(todo[j + 1])
                if what == "W":
                    widen(q)
                elif what == "I":
                    if q == 3:
                        inter_w1()
                    else:
                        interleave(q, False)
                elif what == "J":
                    interleave(q, True)
                elif what == "Q":
                    if q == 3:
                        quant_w1()
                    else:
                        quant_feat(q)

        done_sq = [0]
        for s in range(NS + EXTRA):
            ahead = ahead_of.get(s, [])
            for token, lag in ORDER:
                k = s - lag
                name, i = (token[:-1], int(token[-1])) if token[-1] in "012" else (token, 0)
                if token == "f0":
                    name, i = token, 0
                if name == "sq":
                    n = len(ahead)
                    for g, w, lo, hi in ahead[i * n // 3 : (i + 1) * n // 3]:
                        squares(g, [w], lo, hi)
                    continue
                if name == "prep":
                    prep_step(s)
                    continue
                if not live(k):
                    continue
                q = STEPS[k][1]
                if name == "turn":
                    turn(k, i)
                elif name == "min":
                    minimum(k, i)
                elif name == "exp":
                    expo(k, i)
                elif name == "dist":
                    if k > 0:
                        dist(k, i)
                elif name == "norm":
                    norm(k, i)
                elif name == "recip":
                    recip(k)
                elif name == "gain":
                    gain(k, i)
                elif name == "quanta":
                    quant_a(k)
                elif name == "feats":
                    feats(k)
                elif name == "f0":
                    if q == 0:
                        product(k, 0)
                elif name == "gz":
                    if q > 0:
                        product(k, i)
                elif q == 2:
                    key = pair_of(k)
                    if name == "quantz":
                        quant_z(key)
                    elif name == "linear":
                        linear(key)
                    elif name == "bias":
                        bias(key)
                    elif name == "clamp":
                        clamp(key)
                    elif name == "expout":
                        if key < N // NP - 1:
                            exp_out(key)

        pairs = N // NP
        for key in range(pairs - 1):
            log_out(key, both)
            finish(key, both)
        exp_out(pairs - 1)
        for i in range(PAIR):
            log_out(pairs - 1, slice(i, i + 1))
            finish(pairs - 1, slice(i, i + 1))
